import numpy as np
import ml_dtypes


def mxq(x, axis, fmt="e4m3"):
    dtype, down = {"e4m3": (ml_dtypes.float8_e4m3fn, 7), "e5m2": (ml_dtypes.float8_e5m2, 14)}[fmt]
    v = np.moveaxis(np.asarray(x, np.float32).astype(ml_dtypes.bfloat16).astype(np.float64), axis, -1)
    blocks = v.reshape(v.shape[:-1] + (-1, 32))
    amax = np.abs(blocks).max(-1, keepdims=True)
    byte = np.maximum(np.where(amax > 0, np.frexp(amax)[1] - 1 + 127, 0) - down, 1)
    scale = np.exp2(byte - 127.0)
    codes = (blocks / scale).astype(np.float32).astype(dtype).astype(np.float64)
    return np.moveaxis((codes * scale).reshape(v.shape), -1, axis)


WIDE = False


def mx_kscale(k):
    if not WIDE:
        return np.ones(k)
    levels = np.array([30, -30])
    if k % 512:
        return np.exp2(np.random.permutation(np.resize(levels, k // 32))).repeat(32)
    a = np.empty((k // 512, 16))
    for p in range(k // 512):
        a[p, :8] = np.random.permutation(np.resize(levels, 8))
        for g in range(8):
            far = levels[np.abs(levels - a[p, g]) >= 10]
            a[p, g + 8] = far[np.random.randint(len(far))]
    return np.exp2(a.ravel()).repeat(32)


BF16 = ml_dtypes.bfloat16


def bf(x):
    return np.asarray(x, np.float32).astype(BF16)


def f64(x):
    return np.asarray(x).astype(np.float64)


E2M1 = np.array([0.0, 0.5, 1.0, 1.5, 2.0, 3.0, 4.0, 6.0, -0.0, -0.5, -1.0, -1.5, -2.0, -3.0, -4.0, -6.0])


def pack_weight(w, fmt):
    k, n = w.shape
    w = f64(bf(w)).reshape(k // 32, 32, n)
    amax = np.abs(w).max(1)
    if fmt == "e4m3":
        byte = np.frexp(amax)[1] - 1 + 127 - 7
    else:
        mant, ex = np.frexp(amax / 6.0)
        byte = np.where(mant > 0.5, ex, ex - 1) + 127
    byte = np.clip(np.where(amax > 0, byte, 1), 1, 254)
    scaled = (w * np.exp2(127.0 - byte)[:, None, :]).reshape(k, n).astype(np.float32)
    by_word = np.ascontiguousarray(scaled.reshape(k // 512, 128, 4, n).transpose(0, 1, 3, 2))
    if fmt == "e4m3":
        words = by_word.astype(ml_dtypes.float8_e4m3fn).view(np.uint8)
    else:
        c = by_word.astype(ml_dtypes.float4_e2m1fn).view(np.uint8) & 0xF
        words = c[..., 0::2] | (c[..., 1::2] << 4)
    return np.ascontiguousarray(words), np.ascontiguousarray(byte.astype(np.uint8).reshape(k // 512, 16, n))


def unpack_weight(words, scales, fmt):
    g, p, n, _ = words.shape
    if fmt == "e4m3":
        vals = np.ascontiguousarray(words).view(ml_dtypes.float8_e4m3fn).astype(np.float64)
    else:
        nib = np.empty((g, p, n, 4), np.uint8)
        nib[..., 0::2] = words & 0xF
        nib[..., 1::2] = words >> 4
        vals = E2M1[nib]
    vals = vals * np.repeat(np.exp2(scales.astype(np.float64) - 127.0), 8, axis=1)[..., None]
    return vals.transpose(0, 1, 3, 2).reshape(g * 512, n)
def pack4(w):
    words, scales = pack_weight(w, "e2m1")
    return words.reshape(words.shape[0], 128, -1), scales


def unpack4(words, scales):
    return unpack_weight(words.reshape(words.shape[0], 128, -1, 2), scales, "e2m1")


D, M, R = 4096, 1024, 512


def setup_inputs():
    s = mx_kscale(M)
    c = mx_kscale(D)
    x_next = np.random.standard_normal((D, M)) * s
    v = np.random.standard_normal((M, R)) / np.sqrt(M) / s[:, None]
    v_words, v_scales = pack4(v)
    sigma = 0.5 + 1.5 * np.random.random(R)
    cell = np.exp(0.5 * np.random.standard_normal(D)) * c
    u = np.random.standard_normal((D, R)) / np.sqrt(D) / c[:, None]
    return {"x_next": bf(x_next),
            "v_words": v_words,
            "v_scales": v_scales,
            "sigma": bf(sigma),
            "cell": bf(cell),
            "u": bf(u)}


def reference(x_next, v_words, v_scales, sigma, cell, u):
    v = unpack4(v_words, v_scales)
    xv = mxq(f64(x_next), 1, "e4m3") @ v
    y = xv / f64(sigma)[None, :] * f64(cell)[:, None]
    a = mxq(f64(u), 0, "e4m3").T @ mxq(y, 0, "e5m2")
    return a

from contextlib import ExitStack

import concourse.mybir as mybir
from concourse.masks import make_identity

D, M, R = 4096, 1024, 512
FLOPS = 2 * D * M * R + 2 * D * R * R

F32 = mybir.dt.float32
BF16 = mybir.dt.bfloat16
I32 = mybir.dt.int32
U32 = mybir.dt.uint32
U8 = mybir.dt.uint8
E4M3 = mybir.dt.float8_e4m3fn_x4
E5M2 = mybir.dt.float8_e5m2_x4
E2M1 = mybir.dt.float4_e2m1fn_x4
MULT = mybir.AluOpType.mult
ADD = mybir.AluOpType.add

P = 128
PACK = 4
K_PASS = P * PACK
GROUPS = D // K_PASS
X_PASSES = M // K_PASS
OUT_TILES = R // P
U_COLS_GPSIMD = 384
Y_COLS_VECTOR_LAST = 336
Y_QUANT_LAG = 3
EARLY_GROUPS = 2
GROUP_MAJOR = 6


def tile_dynamic_mode_projection_s9_kernel(tc, x_next, v_words, v_scales, sigma, cell, u, out):
    nc = tc.nc
    with ExitStack() as ctx:
        keep = ctx.enter_context(tc.tile_pool(name="keep", bufs=1))
        work = ctx.enter_context(tc.tile_pool(name="work", bufs=4))
        psum = ctx.enter_context(tc.psum_pool(name="psum", bufs=1))
        ctx.enter_context(tc.manual_schedule())

        ident = keep.tile([P, P], F32, name="ident")
        make_identity(nc, ident[:])
        v_plane = keep.tile([P, X_PASSES, R], U8, name="v_plane", align_bytes=64)
        nc.vector.memset(v_plane[:].rearrange("p g n -> p (g n)").bitcast(I32), 0)

        x_rows = {}

        def load_x(first, count):
            group, slot = divmod(first, PACK)
            tile = keep.tile([P, count, M], BF16, name="x_%d" % first)
            rows = x_next[group * K_PASS:(group + 1) * K_PASS, :].rearrange("(p t) k -> p t k", t=PACK)
            nc.sync.dma_start(out=tile[:], in_=rows[:, slot:slot + count, :])
            for i in range(count):
                x_rows[first + i] = tile[:, i, :]

        u_rows = {}

        def load_u(group):
            tile = keep.tile([P, PACK, R], BF16, name="u_%d" % group)
            rows = u[group * K_PASS:(group + 1) * K_PASS, :].rearrange("(p t) r -> p t r", t=PACK)
            nc.sync.dma_start(out=tile[:], in_=rows)
            u_rows[group] = tile

        load_x(0, 1)
        load_x(1, 1)
        load_x(2, 2)
        for quad in range(4):
            nc.sync.dma_start(
                out=v_plane[32 * quad:32 * quad + 4, :, :].bitcast(I32),
                in_=v_scales[:, 4 * quad:4 * quad + 4, :].rearrange("g q n -> q g n").bitcast(I32),
            )
        sigma_sb = keep.tile([P, PACK], BF16, name="sigma_sb")
        nc.sync.dma_start(out=sigma_sb[:], in_=sigma.rearrange("(p c) -> p c", c=PACK))
        load_x(4, 2)
        v_codes = keep.tile([P, X_PASSES, 2 * R], U8, name="v_codes", align_bytes=64)
        nc.sync.dma_start(out=v_codes[:].bitcast(I32), in_=v_words.rearrange("g p n -> p g n").bitcast(I32))
        load_x(6, 2)
        cell_sb = keep.tile([P, GROUPS, PACK], BF16, name="cell_sb")
        nc.sync.dma_start(out=cell_sb[:], in_=cell.rearrange("(g p t) -> p g t", p=P, t=PACK))
        for group in range(GROUPS):
            load_u(group)
            if group + 2 < GROUPS:
                load_x(PACK * (group + 2), 2)
                load_x(PACK * (group + 2) + 2, 2)

        inv_sigma = keep.tile([P, R], F32, name="inv_sigma")

        def spread_inv_sigma():
            inv_cols = keep.tile([P, PACK], F32, name="inv_cols")
            nc.vector.reciprocal(out=inv_cols[:], in_=sigma_sb[:])
            bank = psum.tile([P, PACK, P], F32, name="spread", tag="y_bank0")
            for c in range(PACK):
                nc.tensor.transpose(bank[:, c, :], inv_cols[:, c:c + 1].to_broadcast([P, P]), ident[:])
            nc.vector.tensor_copy(out=inv_sigma[:].rearrange("p (n c) -> p n c", c=PACK),
                                  in_=bank[:].rearrange("p c n -> p n c"))

        x_packed, x_codes, x_scales = {}, {}, {}

        def turn_x(j):
            bank = psum.tile([P, X_PASSES, 2, P], F32, name="xt", tag="x_bank%d" % (j % PACK))
            words = x_rows[j].bitcast(F32)
            for g in range(X_PASSES):
                for h in range(2):
                    nc.tensor.transpose(bank[:, g, h, :], words[:, 256 * g + h:256 * (g + 1):2], ident[:])
            pair, i = divmod(j, 2)
            if i == 0:
                x_packed[pair] = work.tile([P, 2 * M], BF16, name="x_packed", align_bytes=64)
            dst = x_packed[pair][:, i * M:(i + 1) * M].bitcast(F32)
            nc.scalar.copy(out=dst.rearrange("p (g r h) -> p g r h", g=X_PASSES, h=2),
                           in_=bank[:].rearrange("p g h r -> p g r h"))

        def quantize_x(pair):
            x_codes[pair] = work.tile([P, R], U32, name="x_codes", align_bytes=64)
            x_scales[pair] = work.tile([P, R], U8, name="x_scales", align_bytes=64)
            nc.vector.quantize_mx(out=x_codes[pair][:].bitcast(E4M3), scales=x_scales[pair][:],
                                  in_=x_packed[pair][:])

        y_rows = {}

        def first_product(j):
            group, t = divmod(j, PACK)
            pair, i = divmod(j, 2)
            bank = psum.tile([P, R], F32, name="xv", tag="y_bank%d" % t)
            for g in range(X_PASSES):
                cols = slice((X_PASSES * i + g) * P, (X_PASSES * i + g + 1) * P)
                nc.tensor.matmul_mx(
                    out=bank[:],
                    lhsT=x_codes[pair][:, cols].bitcast(E4M3), lhsT_scale=x_scales[pair][:, cols],
                    rhs=v_codes[:, g, :].bitcast(E2M1), rhs_scale=v_plane[:, g, :],
                    start=(g == 0), stop=(g == X_PASSES - 1),
                )
            if t == 0:
                y_rows[group] = work.tile([P, PACK, R], BF16, name="y_rows", bufs=3)
            nc.vector.scalar_tensor_tensor(out=y_rows[group][:, t, :], in0=bank[:],
                                           scalar=cell_sb[:, group, t:t + 1], in1=inv_sigma[:],
                                           op0=MULT, op1=MULT)

        def by_lines(packed, rows, first, last):
            dst = packed[:, PACK * first:PACK * last].rearrange("p (c i t) -> p c t i", i=4, t=PACK)
            src = rows[:, :, first:last].rearrange("p t (c i) -> p c t i", i=4)
            return dst, src

        y_packed = {}

        def pack_y(group, vector_cols):
            y_packed[group] = work.tile([P, PACK * R], BF16, name="y_packed", bufs=Y_QUANT_LAG + 2, align_bytes=64)
            if vector_cols:
                dst, src = by_lines(y_packed[group], y_rows[group], 0, vector_cols)
                nc.vector.tensor_copy(out=dst, in_=src)
            dst, src = by_lines(y_packed[group], y_rows[group], vector_cols, R)
            nc.scalar.copy(out=dst, in_=src)

        y_codes, y_scales = {}, {}

        def quantize_y(group):
            y_codes[group] = keep.tile([P, R], U32, name="y_codes%d" % group, align_bytes=64)
            y_scales[group] = keep.tile([P, R], U8, name="y_scales%d" % group, align_bytes=64)
            nc.vector.quantize_mx(out=y_codes[group][:].bitcast(E5M2), scales=y_scales[group][:],
                                  in_=y_packed[group][:])

        u_packed = {}

        def pack_u(group):
            u_packed[group] = work.tile([P, PACK * R], BF16, name="u_packed", bufs=1, align_bytes=64)
            nc.gpsimd.tensor_scalar(
                out=u_packed[group][:, :PACK * U_COLS_GPSIMD].rearrange("p (n t) -> p n t", t=PACK),
                in0=u_rows[group][:, :, :U_COLS_GPSIMD].rearrange("p t n -> p n t"),
                scalar1=1.0, scalar2=0.0, op0=MULT, op1=ADD)
            dst, src = by_lines(u_packed[group], u_rows[group], U_COLS_GPSIMD, R)
            nc.scalar.copy(out=dst, in_=src)

        u_codes, u_scales = {}, {}

        def quantize_u(group):
            u_codes[group] = keep.tile([P, R], U32, name="u_codes%d" % group, align_bytes=64)
            u_scales[group] = keep.tile([P, R], U8, name="u_scales%d" % group, align_bytes=64)
            nc.vector.quantize_mx(out=u_codes[group][:].bitcast(E4M3), scales=u_scales[group][:],
                                  in_=u_packed[group][:])

        sums = {}

        def second_product(group, m):
            if group == 0:
                sums[m] = psum.tile([P, R], F32, name="sums", tag="x_bank%d" % m)
            cols = slice(m * P, (m + 1) * P)
            nc.tensor.matmul_mx(
                out=sums[m][:],
                lhsT=u_codes[group][:, cols].bitcast(E4M3), lhsT_scale=u_scales[group][:, cols],
                rhs=y_codes[group][:].bitcast(E5M2), rhs_scale=y_scales[group][:],
                start=(group == 0), stop=(group == GROUPS - 1),
            )

        def store(m):
            result = work.tile([P, R], F32, name="result")
            if m % 2 == 0:
                nc.scalar.copy(out=result[:], in_=sums[m][:])
            else:
                nc.vector.tensor_copy(out=result[:], in_=sums[m][:])
            nc.sync.dma_start(out=out[m * P:(m + 1) * P, :], in_=result[:])

        for step in range(GROUPS + 1):
            if step < GROUPS:
                for j in range(PACK * step, PACK * (step + 1)):
                    turn_x(j)
            if step == 0:
                spread_inv_sigma()
            if step >= 1:
                pack_u(step - 1)
            if step >= 2:
                pack_y(step - 2, 0)
            if step == GROUPS:
                for group in range(EARLY_GROUPS):
                    for m in range(OUT_TILES):
                        second_product(group, m)
            if step >= 1:
                for j in range(PACK * (step - 1), PACK * step):
                    first_product(j)
            if step < GROUPS:
                quantize_x(2 * step)
                quantize_x(2 * step + 1)
            if step >= Y_QUANT_LAG:
                quantize_y(step - Y_QUANT_LAG)
            if step >= 1:
                quantize_u(step - 1)
        pack_y(GROUPS - 1, Y_COLS_VECTOR_LAST)
        for group in range(GROUPS + 1 - Y_QUANT_LAG, GROUPS):
            quantize_y(group)
        for group in range(EARLY_GROUPS, GROUP_MAJOR):
            for m in range(OUT_TILES):
                second_product(group, m)
        for m in range(OUT_TILES):
            for group in range(GROUP_MAJOR, GROUPS):
                second_product(group, m)
            store(m)
